import numpy as np
import ml_dtypes


def mxq(x, axis, fmt="e4m3"):
    dtype, down = {"e4m3": (ml_dtypes.float8_e4m3fn, 7), "e5m2": (ml_dtypes.float8_e5m2, 14)}[fmt]
    v = np.moveaxis(np.asarray(x, np.float32).astype(ml_dtypes.bfloat16).astype(np.float64), axis, -1)
    blocks = v.reshape(v.shape[:-1] + (-1, 32))
    amax = np.abs(blocks).max(-1, keepdims=True)
    byte = np.maximum(np.where(amax > 0, np.frexp(amax)[1] - 1 + 127, 0) - down, 1)
    scale = np.exp2(byte - 127.0)
    codes = (blocks / scale).astype(np.float32).astype(dtype).astype(np.float64)
    return np.moveaxis((codes * scale).reshape(v.shape), -1, axis)


WIDE = False


def mx_kscale(k):
    if not WIDE:
        return np.ones(k)
    levels = np.array([10, -10, 5, -5, 0])
    if k % 512:
        return np.exp2(np.random.permutation(np.resize(levels, k // 32))).repeat(32)
    a = np.empty((k // 512, 16))
    for p in range(k // 512):
        a[p, :8] = np.random.permutation(np.resize(levels, 8))
        for g in range(8):
            far = levels[np.abs(levels - a[p, g]) >= 10]
            a[p, g + 8] = far[np.random.randint(len(far))]
    return np.exp2(a.ravel()).repeat(32)


def f64(x):
    return np.asarray(x).astype(np.float64)


def striped(idx):
    return np.tile(idx.reshape(-1, 16).T, (8, 1)).astype(np.uint16)


def unstriped(offs):
    return offs[:16].T.reshape(-1).astype(np.int64)


E2M1 = np.array([0.0, 0.5, 1.0, 1.5, 2.0, 3.0, 4.0, 6.0, -0.0, -0.5, -1.0, -1.5, -2.0, -3.0, -4.0, -6.0])


def pack_weight(w, fmt):
    k, n = w.shape
    w = f64(np.asarray(w, np.float32).astype(ml_dtypes.bfloat16)).reshape(k // 32, 32, n)
    amax = np.abs(w).max(1)
    if fmt == "e4m3":
        byte = np.frexp(amax)[1] - 1 + 127 - 7
    else:
        mant, ex = np.frexp(amax / 6.0)
        byte = np.where(mant > 0.5, ex, ex - 1) + 127
    byte = np.clip(np.where(amax > 0, byte, 1), 1, 254)
    scaled = (w * np.exp2(127.0 - byte)[:, None, :]).reshape(k, n).astype(np.float32)
    by_word = np.ascontiguousarray(scaled.reshape(k // 512, 128, 4, n).transpose(0, 1, 3, 2))
    if fmt == "e4m3":
        words = by_word.astype(ml_dtypes.float8_e4m3fn).view(np.uint8)
    else:
        c = by_word.astype(ml_dtypes.float4_e2m1fn).view(np.uint8) & 0xF
        words = (c[..., 0::2] | (c[..., 1::2] << 4)).reshape(k // 512, 128, 2 * n)
    return np.ascontiguousarray(words), np.ascontiguousarray(byte.astype(np.uint8).reshape(k // 512, 16, n))


def unpack_weight(words, scales, fmt):
    g, _, n = scales.shape
    words = np.ascontiguousarray(words).reshape(g, 128, n, -1)
    if fmt == "e4m3":
        vals = words.view(ml_dtypes.float8_e4m3fn).astype(np.float64)
    else:
        nib = np.empty((g, 128, n, 4), np.uint8)
        nib[..., 0::2] = words & 0xF
        nib[..., 1::2] = words >> 4
        vals = E2M1[nib]
    vals = vals * np.repeat(np.exp2(scales.astype(np.float64) - 127.0), 8, axis=1)[..., None]
    return vals.transpose(0, 1, 3, 2).reshape(g * 512, n)


def gelu(v):
    return 0.5 * v * (1.0 + np.tanh(np.sqrt(2.0 / np.pi) * (v + 0.044715 * v**3)))


K, K2, H, N, T, T2, S = 1024, 512, 1024, 512, 2048, 4096, 1024

def setup_inputs():
    n = np.random.standard_normal
    s, s2, u = mx_kscale(K)[:, None], mx_kscale(K2)[:, None], mx_kscale(H)[:, None]
    tab_words, tab_scales = pack_weight(n((K, T)) * s, "e4m3")
    tab2_words, tab2_scales = pack_weight(n((K2, T2)) * s2, "e4m3")
    w2_words, w2_scales = pack_weight(n((K2, H)) / np.sqrt(K2) / s2, "e2m1")
    return {
        "tab_words": tab_words, "tab_scales": tab_scales,
        "offs": striped(np.random.permutation(T)[:S]),
        "tab2_words": tab2_words, "tab2_scales": tab2_scales,
        "offs2": striped(np.random.permutation(T2)[:S]),
        "w1": (n((K, H)) / np.sqrt(K) / s).astype(np.float32),
        "w2_words": w2_words, "w2_scales": w2_scales,
        "gain": (np.exp(0.3 * n(H)) * u[:, 0]).astype(np.float32),
        "w3": (n((H, N)) / np.sqrt(H) / u).astype(np.float32),
        "bias": (0.5 * n(N)).astype(np.float32),
    }

def reference(tab_words, tab_scales, offs, tab2_words, tab2_scales, offs2,
              w1, w2_words, w2_scales, gain, w3, bias):
    v = unpack_weight(tab_words, tab_scales, "e4m3")[:, unstriped(offs)]
    v2 = unpack_weight(tab2_words, tab2_scales, "e4m3")[:, unstriped(offs2)]
    w1q = mxq(f64(w1), 0, "e4m3")
    w2 = unpack_weight(w2_words, w2_scales, "e2m1")
    p = w1q.T @ v
    q = w2.T @ v2
    h = f64(gain)[:, None] / (1.0 + np.square(p - q))
    hq = mxq(h, 0, "e4m3")
    w3q = mxq(f64(w3), 0, "e4m3")
    return (w3q.T @ hq) + f64(bias)[:, None]

@@ -1,0 +1,277 @@
+from contextlib import ExitStack
+
+import concourse.mybir as mybir
+
+K, K2, H, N, T, T2, S = 1024, 512, 1024, 512, 2048, 4096, 1024
+FLOPS = 2 * S * (K * H + K2 * H + H * N)
+
+F32 = mybir.dt.float32
+BF16 = mybir.dt.bfloat16
+I32 = mybir.dt.int32
+U32 = mybir.dt.uint32
+U16 = mybir.dt.uint16
+U8 = mybir.dt.uint8
+FP8X4 = mybir.dt.float8_e4m3fn_x4
+FP4X4 = mybir.dt.float4_e2m1fn_x4
+ALU = mybir.AluOpType
+ACT = mybir.ActivationFunctionType
+
+P = 128
+PACK = 4
+PASS = P * PACK
+HALF = 512
+TAB_ROW = (4, 8)
+TINY = 1e-37
+
+
+def tile_list_visual_rerank_pairs_kernel(
+    tc, tab_words, tab_scales, offs, tab2_words, tab2_scales, offs2, w1, w2_words, w2_scales, gain, w3, bias, out
+):
+    nc = tc.nc
+    with ExitStack() as ctx:
+        keep = ctx.enter_context(tc.tile_pool(name="keep", bufs=1))
+        sq_pool = ctx.enter_context(tc.tile_pool(name="sq", bufs=4))
+        ring = ctx.enter_context(tc.tile_pool(name="ring", bufs=3))
+        diff_psum = ctx.enter_context(tc.psum_pool(name="diff", bufs=4))
+        out_psum = ctx.enter_context(tc.psum_pool(name="score", bufs=4))
+
+        def held(shape, dtype, name):
+            return keep.tile(shape, dtype, name=name, align_bytes=64)
+
+        idx = held([P, S // 16], U16, "idx")
+        idx2 = held([P, S // 16], U16, "idx2")
+        tab_w = [held([P, T], I32, "tab_w%d" % a) for a in range(2)]
+        tab_s = held([P, T // 4], I32, "tab_s")
+        tab2_w = held([P, T2], I32, "tab2_w")
+        tab2_s = held([P, T2 // 4], I32, "tab2_s")
+        w2_w_raw = held([P, H // 2], I32, "w2_w_raw")
+        w2_s_raw = held([P, H // 4], I32, "w2_s_raw")
+        w2_w = held([P, 2 * H], U8, "w2_w")
+        w2_s = held([P, H], U8, "w2_s")
+        v_w = [held([P, S], U32, "v_w%d" % a) for a in range(2)]
+        v_s = held([P, S], U8, "v_s")
+        v2_w = held([P, S], U32, "v2_w")
+        v2_s = held([P, S], U8, "v2_s")
+        w1_raw = [[held([P, PACK, PASS], F32, "w1_raw%d%d" % (g, a)) for a in range(2)] for g in range(2)]
+        w1_bf = [[held([P, PASS * PACK], BF16, "w1_bf%d%d" % (g, a)) for a in range(2)] for g in range(2)]
+        w1_w = [[held([P, PASS], U32, "w1_w%d%d" % (g, a)) for a in range(2)] for g in range(2)]
+        w1_s = [[held([P, PASS], U8, "w1_s%d%d" % (g, a)) for a in range(2)] for g in range(2)]
+        w3_raw = [held([P, PACK, N], F32, "w3_raw%d" % g) for g in range(2)]
+        w3_bf = [held([P, N * PACK], BF16, "w3_bf%d" % g) for g in range(2)]
+        w3_w = [held([P, N], U32, "w3_w%d" % g) for g in range(2)]
+        w3_s = [held([P, N], U8, "w3_s%d" % g) for g in range(2)]
+        h_w = [held([P, S], U32, "h_w%d" % g) for g in range(2)]
+        h_s = [held([P, S], U8, "h_s%d" % g) for g in range(2)]
+        gain_sb = held([P, 2, PACK], F32, "gain_sb")
+        gain_abs = held([P, 2 * PACK], F32, "gain_abs")
+        gain_inv = held([P, 2 * PACK], F32, "gain_inv")
+        gain_pos = held([P, 2 * PACK], F32, "gain_pos")
+        gain_sign = held([P, 2 * PACK], F32, "gain_sign")
+        bias_sb = held([P, N // P], F32, "bias_sb")
+        warm_in = held([P, 1], F32, "warm_in")
+        warm_out = held([P, 1], F32, "warm_out")
+        scores = [held([P, N // P, HALF], F32, "scores%d" % hf) for hf in range(2)]
+
+        nc.vector.memset(warm_in[:], 1.0)
+        nc.scalar.activation(warm_out[:], warm_in[:], ACT.Abs_reciprocal_sqrt)
+        nc.vector.memset(tab_s[:], 0)
+        nc.vector.memset(w2_s_raw[:], 0)
+        nc.vector.memset(tab2_s[:], 0)
+
+        def load_w1(g, a):
+            rows = w1[PASS * a : PASS * (a + 1), PASS * g : PASS * (g + 1)]
+            nc.sync.dma_start(w1_raw[g][a][:], rows.rearrange("(p j) c -> p j c", j=PACK))
+
+        def load_words(tile, words):
+            nc.sync.dma_start(tile[:], words.rearrange("p t i -> p (t i)").bitcast(I32))
+
+        load_words(tab_w[0], tab_words[0])
+        nc.sync.dma_start(idx[:], offs)
+        nc.sync.dma_start(idx2[:], offs2)
+        for q in range(4):
+            row = 32 * q + TAB_ROW[0]
+            nc.sync.dma_start(tab_s[row : row + 8, :], tab_scales[:, 4 * q : 4 * q + 4, :].bitcast(I32))
+        load_w1(0, 0)
+        load_words(tab_w[1], tab_words[1])
+        for q in range(4):
+            nc.sync.dma_start(tab2_s[32 * q : 32 * q + 4, :], tab2_scales[0, 4 * q : 4 * q + 4, :].bitcast(I32))
+        nc.sync.dma_start(w2_w_raw[:], w2_words[0].bitcast(I32))
+        load_w1(0, 1)
+        load_words(tab2_w, tab2_words[0])
+        with nc.allow_non_contiguous_dma(reason="four gains a partition"):
+            nc.sync.dma_start(gain_sb[:], gain.rearrange("(g p t) -> p g t", g=2, t=PACK))
+        load_w1(1, 0)
+        load_w1(1, 1)
+        for g in range(2):
+            rows = w3[PASS * g : PASS * (g + 1), :]
+            nc.sync.dma_start(w3_raw[g][:], rows.rearrange("(p j) n -> p j n", j=PACK))
+        for q in range(4):
+            nc.gpsimd.dma_start(w2_s_raw[32 * q : 32 * q + 4, :], w2_scales[0, 4 * q : 4 * q + 4, :].bitcast(I32))
+        with nc.allow_non_contiguous_dma(reason="one bias a partition"):
+            nc.sync.dma_start(bias_sb[:], bias.rearrange("(b p) -> p b", p=P))
+
+        def quantize(words, scales, values):
+            nc.vector.quantize_mx(out=words.bitcast(FP8X4), scales=scales, in_=values)
+
+        def cast_w1(g, a, on_scalar):
+            dst = w1_bf[g][a][:].rearrange("p (t m j) -> p m j t", t=PACK, j=PACK)
+            src = w1_raw[g][a][:].rearrange("p j (m t) -> p m j t", t=PACK)
+            if on_scalar:
+                nc.scalar.activation(dst, src, ACT.Copy, scale=-1.0)
+            else:
+                nc.vector.tensor_scalar(dst, src, -1.0, None, ALU.mult)
+
+        def quantize_w1(g, a):
+            quantize(w1_w[g][a][:], w1_s[g][a][:], w1_bf[g][a][:])
+
+        def cast_w3(g):
+            dst = w3_bf[g][:].rearrange("p (c i j) -> p c j i", i=4, j=PACK)
+            src = w3_raw[g][:].rearrange("p j (c i) -> p c j i", i=4)
+            sign = gain_sign[:, PACK * g : PACK * (g + 1)].unsqueeze(1).unsqueeze(3).broadcast_to([P, N // 4, PACK, 4])
+            nc.vector.tensor_tensor(dst, src, sign, ALU.mult)
+
+        def gather(dst, window, offsets, hf):
+            cols = slice(HALF * hf, HALF * (hf + 1))
+            nc.vector.tensor_copy(dst[:, cols], window.indirect(offsets[:, HALF // 16 * hf : HALF // 16 * (hf + 1)]))
+
+        roots = {}
+
+        def difference(g, hf, t):
+            cols = slice(HALF * hf, HALF * (hf + 1))
+            chan = slice(P * t, P * (t + 1))
+            bank = diff_psum.tile([P, HALF], F32, name="bank")
+            for a in range(2):
+                nc.tensor.matmul_mx(
+                    out=bank[:],
+                    lhsT=w1_w[g][a][:, chan].bitcast(FP8X4),
+                    lhsT_scale=w1_s[g][a][:, chan],
+                    rhs=v_w[a][:, cols].bitcast(FP8X4),
+                    rhs_scale=v_s[TAB_ROW[a] : P, cols],
+                    start=(a == 0),
+                    stop=False,
+                )
+            c0 = PASS * g + P * t
+            nc.tensor.matmul_mx(
+                out=bank[:],
+                lhsT=w2_w[:, 2 * c0 : 2 * (c0 + P)].bitcast(FP4X4),
+                lhsT_scale=w2_s[:, c0 : c0 + P],
+                rhs=v2_w[:, cols].bitcast(FP8X4),
+                rhs_scale=v2_s[:, cols],
+                start=False,
+                stop=True,
+            )
+            square = sq_pool.tile([P, HALF], F32, name="square")
+            nc.scalar.activation(square[:], bank[:], ACT.Square)
+            return square
+
+        def root(g, hf, t, square, lo, hi):
+            col = gain_inv[:, PACK * g + t : PACK * g + t + 1]
+            nc.scalar.activation(roots[g, hf][:, t, lo:hi], square[:, lo:hi], ACT.Abs_reciprocal_sqrt, bias=col, scale=col)
+
+        def similarity(g, hf, lo, hi):
+            values = ring.tile([P, (hi - lo) * PACK], BF16, name="values", align_bytes=64)
+            src = roots[g, hf][:, :, lo:hi].rearrange("p t (c i) -> p c t i", i=4)
+            nc.vector.tensor_tensor(values[:].rearrange("p (c i t) -> p c t i", i=4, t=PACK), src, src, ALU.mult)
+            return values
+
+        def quantize_h(g, hf, lo, hi, values):
+            cols = slice(HALF * hf + lo, HALF * hf + hi)
+            quantize(h_w[g][:, cols], h_s[g][:, cols], values[:])
+
+        def score(hf, lo, hi, engines):
+            cols = slice(HALF * hf + lo, HALF * hf + hi)
+            for b in range(N // P):
+                acc = out_psum.tile([P, hi - lo], F32, name="acc")
+                for g in range(2):
+                    nc.tensor.matmul_mx(
+                        out=acc[:],
+                        lhsT=w3_w[g][:, P * b : P * (b + 1)].bitcast(FP8X4),
+                        lhsT_scale=w3_s[g][:, P * b : P * (b + 1)],
+                        rhs=h_w[g][:, cols].bitcast(FP8X4),
+                        rhs_scale=h_s[g][:, cols],
+                        start=(g == 0),
+                        stop=(g == 1),
+                    )
+                if engines[b] == "s":
+                    nc.scalar.activation(scores[hf][:, b, lo:hi], acc[:], ACT.Identity, bias=bias_sb[:, b : b + 1])
+                else:
+                    nc.vector.tensor_scalar(scores[hf][:, b, lo:hi], acc[:], bias_sb[:, b : b + 1], None, ALU.add)
+                if b % 2 == 1:
+                    nc.sync.dma_start(
+                        out.rearrange("(b p) s -> p b s", p=P)[:, b - 1 : b + 1, cols], scores[hf][:, b - 1 : b + 1, lo:hi]
+                    )
+
+        def unit(g, hf, pieces):
+            roots[g, hf] = ring.tile([P, PACK, HALF], F32, name="root")
+            lo, hi = pieces[0]
+            squares = []
+            for t in range(PACK):
+                squares.append(difference(g, hf, t))
+                if t > 0:
+                    root(g, hf, t - 1, squares[t - 1], lo, hi)
+            root(g, hf, PACK - 1, squares[PACK - 1], lo, hi)
+            for lo, hi in pieces[1:]:
+                for t in range(PACK):
+                    root(g, hf, t, squares[t], lo, hi)
+
+        def prepare_gain():
+            gain_flat = gain_sb[:].rearrange("p g t -> p (g t)")
+            nc.vector.scalar_tensor_tensor(gain_abs[:], gain_flat, -1.0, gain_flat, ALU.mult, ALU.max)
+            nc.vector.tensor_scalar(gain_pos[:], gain_flat, 0.0, 2.0, ALU.is_ge, ALU.mult)
+            nc.vector.tensor_scalar(gain_abs[:], gain_abs[:], TINY, None, ALU.max)
+            nc.vector.tensor_scalar(gain_sign[:], gain_pos[:], -1.0, None, ALU.add)
+            nc.vector.reciprocal(gain_inv[:], gain_abs[:])
+
+        def reorder_w2():
+            nc.vector.tensor_copy(
+                w2_w[:].bitcast(U16).rearrange("p (g t m) -> p g m t", g=2, t=PACK),
+                w2_w_raw[:].bitcast(U16).rearrange("p (g m t) -> p g m t", g=2, t=PACK),
+            )
+            nc.vector.tensor_copy(
+                w2_s[:].rearrange("p (g t m) -> p g m t", g=2, t=PACK),
+                w2_s_raw[:].bitcast(U8).rearrange("p (g m t) -> p g m t", g=2, t=PACK),
+            )
+
+        cast_w1(0, 0, True)
+        cast_w1(0, 1, True)
+        for hf in range(2):
+            gather(v_w[0], tab_w[0][:].bitcast(U32), idx, hf)
+        for hf in range(2):
+            gather(v_s, tab_s[:].bitcast(U8), idx, hf)
+        quantize_w1(0, 0)
+        gather(v_w[1], tab_w[1][:].bitcast(U32), idx, 0)
+        gather(v2_s, tab2_s[:].bitcast(U8), idx2, 0)
+        reorder_w2()
+        quantize_w1(0, 1)
+        gather(v2_w, tab2_w[:].bitcast(U32), idx2, 0)
+        prepare_gain()
+        gather(v_w[1], tab_w[1][:].bitcast(U32), idx, 1)
+        gather(v2_s, tab2_s[:].bitcast(U8), idx2, 1)
+        gather(v2_w, tab2_w[:].bitcast(U32), idx2, 1)
+
+        whole = [(0, HALF)]
+        split = [(0, HALF // 2), (HALF // 2, HALF)]
+
+        unit(0, 0, whole)
+        for a in range(2):
+            cast_w1(1, a, False)
+        for a in range(2):
+            quantize_w1(1, a)
+        unit(0, 1, whole)
+        values00 = similarity(0, 0, 0, HALF)
+        cast_w3(0)
+        quantize_h(0, 0, 0, HALF, values00)
+        unit(1, 0, whole)
+        values01 = similarity(0, 1, 0, HALF)
+        quantize(w3_w[0][:], w3_s[0][:], w3_bf[0][:])
+        cast_w3(1)
+        quantize_h(0, 1, 0, HALF, values01)
+        unit(1, 1, split)
+        values10 = similarity(1, 0, 0, HALF)
+        quantize(w3_w[1][:], w3_s[1][:], w3_bf[1][:])
+        quantize_h(1, 0, 0, HALF, values10)
+        score(0, 0, HALF, "ssss")
+        for (lo, hi), engines in zip(split, ("ssss", "vsvs")):
+            values11 = similarity(1, 1, lo, hi)
+            quantize_h(1, 1, lo, hi, values11)
+            score(1, lo, hi, engines)

@@ -35,8 +35,8 @@ def tile_list_visual_rerank_pairs_kernel(
         diff_psum = ctx.enter_context(tc.psum_pool(name="diff", bufs=4))
         out_psum = ctx.enter_context(tc.psum_pool(name="score", bufs=4))
 
-        def held(shape, dtype, name):
-            return keep.tile(shape, dtype, name=name, align_bytes=64)
+        def held(shape, dtype, name, tag=None):
+            return keep.tile(shape, dtype, name=name, tag=tag or name, align_bytes=64)
 
         idx = held([P, S // 16], U16, "idx")
         idx2 = held([P, S // 16], U16, "idx2")
@@ -52,12 +52,12 @@ def tile_list_visual_rerank_pairs_kernel(
         v_s = held([P, S], U8, "v_s")
         v2_w = held([P, S], U32, "v2_w")
         v2_s = held([P, S], U8, "v2_s")
-        w1_raw = [[held([P, PACK, PASS], F32, "w1_raw%d%d" % (g, a)) for a in range(2)] for g in range(2)]
-        w1_bf = [[held([P, PASS * PACK], BF16, "w1_bf%d%d" % (g, a)) for a in range(2)] for g in range(2)]
+        w1_raw = {(g, a): held([P, PACK, PASS], F32, "w1_raw%d%d" % (g, a)) for g in range(2) for a in range(2)}
+        w3_raw = [held([P, PACK, N], F32, "w3_raw%d" % g) for g in range(2)]
+        w1_bf = [held([P, 2, PASS * PACK], BF16, "w1_bf0", tag="w1_bf")]
         w1_w = [[held([P, PASS], U32, "w1_w%d%d" % (g, a)) for a in range(2)] for g in range(2)]
         w1_s = [[held([P, PASS], U8, "w1_s%d%d" % (g, a)) for a in range(2)] for g in range(2)]
-        w3_raw = [held([P, PACK, N], F32, "w3_raw%d" % g) for g in range(2)]
-        w3_bf = [held([P, N * PACK], BF16, "w3_bf%d" % g) for g in range(2)]
+        w3_bf = []
         w3_w = [held([P, N], U32, "w3_w%d" % g) for g in range(2)]
         w3_s = [held([P, N], U8, "w3_s%d" % g) for g in range(2)]
         h_w = [held([P, S], U32, "h_w%d" % g) for g in range(2)]
@@ -78,53 +78,54 @@ def tile_list_visual_rerank_pairs_kernel(
         nc.vector.memset(w2_s_raw[:], 0)
         nc.vector.memset(tab2_s[:], 0)
 
-        def load_w1(g, a):
-            rows = w1[PASS * a : PASS * (a + 1), PASS * g : PASS * (g + 1)]
-            nc.sync.dma_start(w1_raw[g][a][:], rows.rearrange("(p j) c -> p j c", j=PACK))
+        def load_w1(g, a, lo, hi):
+            rows = w1[PASS * a : PASS * (a + 1), PASS * g + lo : PASS * g + hi]
+            nc.sync.dma_start(w1_raw[g, a][:, :, lo:hi], rows.rearrange("(p j) c -> p j c", j=PACK))
 
         def load_words(tile, words):
             nc.sync.dma_start(tile[:], words.rearrange("p t i -> p (t i)").bitcast(I32))
 
-        load_words(tab_w[0], tab_words[0])
         nc.sync.dma_start(idx[:], offs)
-        nc.sync.dma_start(idx2[:], offs2)
+        load_words(tab_w[0], tab_words[0])
         for q in range(4):
             row = 32 * q + TAB_ROW[0]
             nc.sync.dma_start(tab_s[row : row + 8, :], tab_scales[:, 4 * q : 4 * q + 4, :].bitcast(I32))
-        load_w1(0, 0)
+        nc.sync.dma_start(idx2[:], offs2)
+        load_w1(0, 0, 0, PASS)
         load_words(tab_w[1], tab_words[1])
         for q in range(4):
             nc.sync.dma_start(tab2_s[32 * q : 32 * q + 4, :], tab2_scales[0, 4 * q : 4 * q + 4, :].bitcast(I32))
+        load_w1(0, 1, 0, PASS)
+        for q in range(4):
+            nc.sync.dma_start(w2_s_raw[32 * q : 32 * q + 4, :], w2_scales[0, 4 * q : 4 * q + 4, :].bitcast(I32))
         nc.sync.dma_start(w2_w_raw[:], w2_words[0].bitcast(I32))
-        load_w1(0, 1)
-        load_words(tab2_w, tab2_words[0])
         with nc.allow_non_contiguous_dma(reason="four gains a partition"):
             nc.sync.dma_start(gain_sb[:], gain.rearrange("(g p t) -> p g t", g=2, t=PACK))
-        load_w1(1, 0)
-        load_w1(1, 1)
+        load_words(tab2_w, tab2_words[0])
+        for a in range(2):
+            load_w1(1, a, 0, PASS)
         for g in range(2):
             rows = w3[PASS * g : PASS * (g + 1), :]
             nc.sync.dma_start(w3_raw[g][:], rows.rearrange("(p j) n -> p j n", j=PACK))
-        for q in range(4):
-            nc.gpsimd.dma_start(w2_s_raw[32 * q : 32 * q + 4, :], w2_scales[0, 4 * q : 4 * q + 4, :].bitcast(I32))
         with nc.allow_non_contiguous_dma(reason="one bias a partition"):
             nc.sync.dma_start(bias_sb[:], bias.rearrange("(b p) -> p b", p=P))
 
         def quantize(words, scales, values):
             nc.vector.quantize_mx(out=words.bitcast(FP8X4), scales=scales, in_=values)
 
-        def cast_w1(g, a, on_scalar):
-            dst = w1_bf[g][a][:].rearrange("p (t m j) -> p m j t", t=PACK, j=PACK)
-            src = w1_raw[g][a][:].rearrange("p j (m t) -> p m j t", t=PACK)
+        def cast_w1(g, a, lo, hi, on_scalar):
+            dst = w1_bf[g][:, a].rearrange("p (t m j) -> p m j t", t=PACK, j=PACK)[:, lo // PACK : hi // PACK]
+            src = w1_raw[g, a][:, :, lo:hi].rearrange("p j (m t) -> p m j t", t=PACK)
             if on_scalar:
                 nc.scalar.activation(dst, src, ACT.Copy, scale=-1.0)
             else:
                 nc.vector.tensor_scalar(dst, src, -1.0, None, ALU.mult)
 
-        def quantize_w1(g, a):
-            quantize(w1_w[g][a][:], w1_s[g][a][:], w1_bf[g][a][:])
+        def quantize_w1(g, a, lo, hi):
+            quantize(w1_w[g][a][:, lo:hi], w1_s[g][a][:, lo:hi], w1_bf[g][:, a, PACK * lo : PACK * hi])
 
         def cast_w3(g):
+            w3_bf.append(held([P, N * PACK], BF16, "w3_bf%d" % g, tag="root0%d" % g))
             dst = w3_bf[g][:].rearrange("p (c i j) -> p c j i", i=4, j=PACK)
             src = w3_raw[g][:].rearrange("p j (c i) -> p c j i", i=4)
             sign = gain_sign[:, PACK * g : PACK * (g + 1)].unsqueeze(1).unsqueeze(3).broadcast_to([P, N // 4, PACK, 4])
@@ -202,7 +203,7 @@ def tile_list_visual_rerank_pairs_kernel(
                     )
 
         def unit(g, hf, pieces):
-            roots[g, hf] = ring.tile([P, PACK, HALF], F32, name="root")
+            roots[g, hf] = held([P, PACK, HALF], F32, "root%d%d" % (g, hf))
             lo, hi = pieces[0]
             squares = []
             for t in range(PACK):
@@ -222,41 +223,38 @@ def tile_list_visual_rerank_pairs_kernel(
             nc.vector.tensor_scalar(gain_sign[:], gain_pos[:], -1.0, None, ALU.add)
             nc.vector.reciprocal(gain_inv[:], gain_abs[:])
 
-        def reorder_w2():
+        def reorder_w2(dst, src):
             nc.vector.tensor_copy(
-                w2_w[:].bitcast(U16).rearrange("p (g t m) -> p g m t", g=2, t=PACK),
-                w2_w_raw[:].bitcast(U16).rearrange("p (g m t) -> p g m t", g=2, t=PACK),
-            )
-            nc.vector.tensor_copy(
-                w2_s[:].rearrange("p (g t m) -> p g m t", g=2, t=PACK),
-                w2_s_raw[:].bitcast(U8).rearrange("p (g m t) -> p g m t", g=2, t=PACK),
+                dst.rearrange("p (g t m) -> p g t m", g=2, t=PACK), src.rearrange("p (g m t) -> p g t m", g=2, t=PACK)
             )
 
-        cast_w1(0, 0, True)
-        cast_w1(0, 1, True)
+        for a in range(2):
+            cast_w1(0, a, 0, PASS, True)
         for hf in range(2):
             gather(v_w[0], tab_w[0][:].bitcast(U32), idx, hf)
         for hf in range(2):
             gather(v_s, tab_s[:].bitcast(U8), idx, hf)
-        quantize_w1(0, 0)
-        gather(v_w[1], tab_w[1][:].bitcast(U32), idx, 0)
-        gather(v2_s, tab2_s[:].bitcast(U8), idx2, 0)
-        reorder_w2()
-        quantize_w1(0, 1)
-        gather(v2_w, tab2_w[:].bitcast(U32), idx2, 0)
+        for hf in range(2):
+            gather(v_w[1], tab_w[1][:].bitcast(U32), idx, hf)
+        quantize_w1(0, 0, 0, PASS)
+        for hf in range(2):
+            gather(v2_s, tab2_s[:].bitcast(U8), idx2, hf)
+        quantize_w1(0, 1, 0, PASS)
+        reorder_w2(w2_w[:].bitcast(U16), w2_w_raw[:].bitcast(U16))
+        reorder_w2(w2_s[:], w2_s_raw[:].bitcast(U8))
         prepare_gain()
-        gather(v_w[1], tab_w[1][:].bitcast(U32), idx, 1)
-        gather(v2_s, tab2_s[:].bitcast(U8), idx2, 1)
-        gather(v2_w, tab2_w[:].bitcast(U32), idx2, 1)
+        for hf in range(2):
+            gather(v2_w, tab2_w[:].bitcast(U32), idx2, hf)
 
+        w1_bf.append(held([P, 2, PASS * PACK], BF16, "w1_bf1", tag="tab2_w"))
         whole = [(0, HALF)]
         split = [(0, HALF // 2), (HALF // 2, HALF)]
 
         unit(0, 0, whole)
         for a in range(2):
-            cast_w1(1, a, False)
+            cast_w1(1, a, 0, PASS, False)
         for a in range(2):
-            quantize_w1(1, a)
+            quantize_w1(1, a, 0, PASS)
         unit(0, 1, whole)
         values00 = similarity(0, 0, 0, HALF)
         cast_w3(0)

@@ -30,33 +30,34 @@ def tile_list_visual_rerank_pairs_kernel(
     nc = tc.nc
     with ExitStack() as ctx:
         keep = ctx.enter_context(tc.tile_pool(name="keep", bufs=1))
+        shared = ctx.enter_context(tc.tile_pool(name="shared", bufs=1))
         sq_pool = ctx.enter_context(tc.tile_pool(name="sq", bufs=4))
-        ring = ctx.enter_context(tc.tile_pool(name="ring", bufs=3))
-        diff_psum = ctx.enter_context(tc.psum_pool(name="diff", bufs=4))
-        out_psum = ctx.enter_context(tc.psum_pool(name="score", bufs=4))
+        ring = ctx.enter_context(tc.tile_pool(name="ring", bufs=4))
+        psum = ctx.enter_context(tc.psum_pool(name="psum", bufs=8))
 
         def held(shape, dtype, name, tag=None):
             return keep.tile(shape, dtype, name=name, tag=tag or name, align_bytes=64)
 
+        def placed(shape, dtype, name, offset):
+            return shared.tile(shape, dtype, name=name, align_bytes=64, offset=offset)
+
         idx = held([P, S // 16], U16, "idx")
         idx2 = held([P, S // 16], U16, "idx2")
         tab_w = [held([P, T], I32, "tab_w%d" % a) for a in range(2)]
-        tab_s = held([P, T // 4], I32, "tab_s")
-        tab2_w = held([P, T2], I32, "tab2_w")
+        tab_s = placed([P, T // 4], I32, "tab_s", 0)
+        tab2_w = placed([P, T2], I32, "tab2_w", 4096)
         tab2_s = held([P, T2 // 4], I32, "tab2_s")
         w2_w_raw = held([P, H // 2], I32, "w2_w_raw")
         w2_s_raw = held([P, H // 4], I32, "w2_s_raw")
         w2_w = held([P, 2 * H], U8, "w2_w")
         w2_s = held([P, H], U8, "w2_s")
-        v_w = [held([P, S], U32, "v_w%d" % a) for a in range(2)]
+        v_w = {(0, hf): held([P, HALF], U32, "v_w0%d" % hf) for hf in range(2)}
         v_s = held([P, S], U8, "v_s")
-        v2_w = held([P, S], U32, "v2_w")
-        v2_s = held([P, S], U8, "v2_s")
-        w1_raw = {(g, a): held([P, PACK, PASS], F32, "w1_raw%d%d" % (g, a)) for g in range(2) for a in range(2)}
+        w1_raw = {}
         w3_raw = [held([P, PACK, N], F32, "w3_raw%d" % g) for g in range(2)]
         w1_bf = [held([P, 2, PASS * PACK], BF16, "w1_bf0", tag="w1_bf")]
-        w1_w = [[held([P, PASS], U32, "w1_w%d%d" % (g, a)) for a in range(2)] for g in range(2)]
-        w1_s = [[held([P, PASS], U8, "w1_s%d%d" % (g, a)) for a in range(2)] for g in range(2)]
+        w1_w = {(g, a): held([P, PASS], U32, "w1_w%d%d" % (g, a)) for g, a in ((0, 0), (1, 0), (1, 1))}
+        w1_s = {(g, a): held([P, PASS], U8, "w1_s%d%d" % (g, a)) for g, a in ((0, 1), (1, 0), (1, 1))}
         w3_bf = []
         w3_w = [held([P, N], U32, "w3_w%d" % g) for g in range(2)]
         w3_s = [held([P, N], U8, "w3_s%d" % g) for g in range(2)]
@@ -70,7 +71,6 @@ def tile_list_visual_rerank_pairs_kernel(
         bias_sb = held([P, N // P], F32, "bias_sb")
         warm_in = held([P, 1], F32, "warm_in")
         warm_out = held([P, 1], F32, "warm_out")
-        scores = [held([P, N // P, HALF], F32, "scores%d" % hf) for hf in range(2)]
 
         nc.vector.memset(warm_in[:], 1.0)
         nc.scalar.activation(warm_out[:], warm_in[:], ACT.Abs_reciprocal_sqrt)
@@ -80,30 +80,32 @@ def tile_list_visual_rerank_pairs_kernel(
 
         def load_w1(g, a, lo, hi):
             rows = w1[PASS * a : PASS * (a + 1), PASS * g + lo : PASS * g + hi]
-            nc.sync.dma_start(w1_raw[g, a][:, :, lo:hi], rows.rearrange("(p j) c -> p j c", j=PACK))
+            w1_raw[g, a, lo] = held([P, PACK, hi - lo], F32, "w1_raw%d%d_%d" % (g, a, lo))
+            nc.sync.dma_start(w1_raw[g, a, lo][:], rows.rearrange("(p j) c -> p j c", j=PACK))
 
         def load_words(tile, words):
             nc.sync.dma_start(tile[:], words.rearrange("p t i -> p (t i)").bitcast(I32))
 
-        nc.sync.dma_start(idx[:], offs)
-        load_words(tab_w[0], tab_words[0])
         for q in range(4):
             row = 32 * q + TAB_ROW[0]
-            nc.sync.dma_start(tab_s[row : row + 8, :], tab_scales[:, 4 * q : 4 * q + 4, :].bitcast(I32))
+            nc.gpsimd.dma_start(tab_s[row : row + 8, :], tab_scales[:, 4 * q : 4 * q + 4, :].bitcast(I32))
+        for r in range(4):
+            nc.gpsimd.dma_start(w2_s_raw[r:P:32, :], w2_scales[0, r:16:4, :].bitcast(I32))
+        for r in range(4):
+            nc.gpsimd.dma_start(tab2_s[r:P:32, :], tab2_scales[0, r:16:4, :].bitcast(I32))
+        with nc.allow_non_contiguous_dma(reason="four gains a partition"):
+            nc.sync.dma_start(gain_sb[:], gain.rearrange("(g p t) -> p g t", g=2, t=PACK))
+        nc.sync.dma_start(w2_w_raw[:], w2_words[0].bitcast(I32))
+        nc.sync.dma_start(idx[:], offs)
+        load_words(tab_w[0], tab_words[0])
         nc.sync.dma_start(idx2[:], offs2)
         load_w1(0, 0, 0, PASS)
         load_words(tab_w[1], tab_words[1])
-        for q in range(4):
-            nc.sync.dma_start(tab2_s[32 * q : 32 * q + 4, :], tab2_scales[0, 4 * q : 4 * q + 4, :].bitcast(I32))
         load_w1(0, 1, 0, PASS)
-        for q in range(4):
-            nc.sync.dma_start(w2_s_raw[32 * q : 32 * q + 4, :], w2_scales[0, 4 * q : 4 * q + 4, :].bitcast(I32))
-        nc.sync.dma_start(w2_w_raw[:], w2_words[0].bitcast(I32))
-        with nc.allow_non_contiguous_dma(reason="four gains a partition"):
-            nc.sync.dma_start(gain_sb[:], gain.rearrange("(g p t) -> p g t", g=2, t=PACK))
         load_words(tab2_w, tab2_words[0])
-        for a in range(2):
-            load_w1(1, a, 0, PASS)
+        load_w1(1, 0, 0, PASS)
+        load_w1(1, 1, 0, PASS // 2)
+        load_w1(1, 1, PASS // 2, PASS)
         for g in range(2):
             rows = w3[PASS * g : PASS * (g + 1), :]
             nc.sync.dma_start(w3_raw[g][:], rows.rearrange("(p j) n -> p j n", j=PACK))
@@ -115,38 +117,37 @@ def tile_list_visual_rerank_pairs_kernel(
 
         def cast_w1(g, a, lo, hi, on_scalar):
             dst = w1_bf[g][:, a].rearrange("p (t m j) -> p m j t", t=PACK, j=PACK)[:, lo // PACK : hi // PACK]
-            src = w1_raw[g, a][:, :, lo:hi].rearrange("p j (m t) -> p m j t", t=PACK)
+            src = w1_raw[g, a, lo][:].rearrange("p j (m t) -> p m j t", t=PACK)
             if on_scalar:
                 nc.scalar.activation(dst, src, ACT.Copy, scale=-1.0)
             else:
                 nc.vector.tensor_scalar(dst, src, -1.0, None, ALU.mult)
 
         def quantize_w1(g, a, lo, hi):
-            quantize(w1_w[g][a][:, lo:hi], w1_s[g][a][:, lo:hi], w1_bf[g][:, a, PACK * lo : PACK * hi])
+            quantize(w1_w[g, a][:, lo:hi], w1_s[g, a][:, lo:hi], w1_bf[g][:, a, PACK * lo : PACK * hi])
 
         def cast_w3(g):
-            w3_bf.append(held([P, N * PACK], BF16, "w3_bf%d" % g, tag="root0%d" % g))
+            w3_bf.append(held([P, N * PACK], BF16, "w3_bf%d" % g, tag="root%d0" % g))
             dst = w3_bf[g][:].rearrange("p (c i j) -> p c j i", i=4, j=PACK)
             src = w3_raw[g][:].rearrange("p j (c i) -> p c j i", i=4)
             sign = gain_sign[:, PACK * g : PACK * (g + 1)].unsqueeze(1).unsqueeze(3).broadcast_to([P, N // 4, PACK, 4])
             nc.vector.tensor_tensor(dst, src, sign, ALU.mult)
 
         def gather(dst, window, offsets, hf):
-            cols = slice(HALF * hf, HALF * (hf + 1))
-            nc.vector.tensor_copy(dst[:, cols], window.indirect(offsets[:, HALF // 16 * hf : HALF // 16 * (hf + 1)]))
+            nc.vector.tensor_copy(dst, window.indirect(offsets[:, HALF // 16 * hf : HALF // 16 * (hf + 1)]))
 
         roots = {}
 
         def difference(g, hf, t):
             cols = slice(HALF * hf, HALF * (hf + 1))
             chan = slice(P * t, P * (t + 1))
-            bank = diff_psum.tile([P, HALF], F32, name="bank")
+            bank = psum.tile([P, HALF], F32, name="bank")
             for a in range(2):
                 nc.tensor.matmul_mx(
                     out=bank[:],
-                    lhsT=w1_w[g][a][:, chan].bitcast(FP8X4),
-                    lhsT_scale=w1_s[g][a][:, chan],
-                    rhs=v_w[a][:, cols].bitcast(FP8X4),
+                    lhsT=w1_w[g, a][:, chan].bitcast(FP8X4),
+                    lhsT_scale=w1_s[g, a][:, chan],
+                    rhs=v_w[a, hf][:].bitcast(FP8X4),
                     rhs_scale=v_s[TAB_ROW[a] : P, cols],
                     start=(a == 0),
                     stop=False,
@@ -169,23 +170,27 @@ def tile_list_visual_rerank_pairs_kernel(
             col = gain_inv[:, PACK * g + t : PACK * g + t + 1]
             nc.scalar.activation(roots[g, hf][:, t, lo:hi], square[:, lo:hi], ACT.Abs_reciprocal_sqrt, bias=col, scale=col)
 
-        def similarity(g, hf, lo, hi):
+        def similarity(g, hf, lo, hi, on_scalar):
             values = ring.tile([P, (hi - lo) * PACK], BF16, name="values", align_bytes=64)
             src = roots[g, hf][:, :, lo:hi].rearrange("p t (c i) -> p c t i", i=4)
-            nc.vector.tensor_tensor(values[:].rearrange("p (c i t) -> p c t i", i=4, t=PACK), src, src, ALU.mult)
+            dst = values[:].rearrange("p (c i t) -> p c t i", i=4, t=PACK)
+            if on_scalar:
+                nc.scalar.activation(dst, src, ACT.Square)
+            else:
+                nc.vector.tensor_tensor(dst, src, src, ALU.mult)
             return values
 
         def quantize_h(g, hf, lo, hi, values):
             cols = slice(HALF * hf + lo, HALF * hf + hi)
             quantize(h_w[g][:, cols], h_s[g][:, cols], values[:])
 
-        def score(hf, lo, hi, engines):
+        def score(hf, lo, hi):
             cols = slice(HALF * hf + lo, HALF * hf + hi)
+            accs = [psum.tile([P, hi - lo], F32, name="bank") for b in range(N // P)]
             for b in range(N // P):
-                acc = out_psum.tile([P, hi - lo], F32, name="acc")
                 for g in range(2):
                     nc.tensor.matmul_mx(
-                        out=acc[:],
+                        out=accs[b][:],
                         lhsT=w3_w[g][:, P * b : P * (b + 1)].bitcast(FP8X4),
                         lhsT_scale=w3_s[g][:, P * b : P * (b + 1)],
                         rhs=h_w[g][:, cols].bitcast(FP8X4),
@@ -193,24 +198,28 @@ def tile_list_visual_rerank_pairs_kernel(
                         start=(g == 0),
                         stop=(g == 1),
                     )
-                if engines[b] == "s":
-                    nc.scalar.activation(scores[hf][:, b, lo:hi], acc[:], ACT.Identity, bias=bias_sb[:, b : b + 1])
-                else:
-                    nc.vector.tensor_scalar(scores[hf][:, b, lo:hi], acc[:], bias_sb[:, b : b + 1], None, ALU.add)
-                if b % 2 == 1:
-                    nc.sync.dma_start(
-                        out.rearrange("(b p) s -> p b s", p=P)[:, b - 1 : b + 1, cols], scores[hf][:, b - 1 : b + 1, lo:hi]
-                    )
+            return accs
 
-        def unit(g, hf, pieces):
+        def emit(hf, lo, hi, accs, engines, group):
+            cols = slice(HALF * hf + lo, HALF * hf + hi)
+            staged = held([P, N // P, hi - lo], F32, "scores%d_%d" % (hf, lo))
+            for b in range(N // P):
+                if engines[b] == "s":
+                    nc.scalar.activation(staged[:, b], accs[b][:], ACT.Identity, bias=bias_sb[:, b : b + 1])
+                else:
+                    nc.vector.tensor_scalar(staged[:, b], accs[b][:], bias_sb[:, b : b + 1], None, ALU.add)
+                if (b + 1) % group == 0:
+                    rows = slice(b + 1 - group, b + 1)
+                    nc.sync.dma_start(out.rearrange("(b p) s -> p b s", p=P)[:, rows, cols], staged[:, rows])
+
+        def unit(g, hf, pieces=((0, HALF),)):
             roots[g, hf] = held([P, PACK, HALF], F32, "root%d%d" % (g, hf))
-            lo, hi = pieces[0]
             squares = []
             for t in range(PACK):
                 squares.append(difference(g, hf, t))
                 if t > 0:
-                    root(g, hf, t - 1, squares[t - 1], lo, hi)
-            root(g, hf, PACK - 1, squares[PACK - 1], lo, hi)
+                    root(g, hf, t - 1, squares[t - 1], *pieces[0])
+            root(g, hf, PACK - 1, squares[PACK - 1], *pieces[0])
             for lo, hi in pieces[1:]:
                 for t in range(PACK):
                     root(g, hf, t, squares[t], lo, hi)
@@ -230,46 +239,58 @@ def tile_list_visual_rerank_pairs_kernel(
 
         for a in range(2):
             cast_w1(0, a, 0, PASS, True)
-        for hf in range(2):
-            gather(v_w[0], tab_w[0][:].bitcast(U32), idx, hf)
-        for hf in range(2):
-            gather(v_s, tab_s[:].bitcast(U8), idx, hf)
-        for hf in range(2):
-            gather(v_w[1], tab_w[1][:].bitcast(U32), idx, hf)
-        quantize_w1(0, 0, 0, PASS)
-        for hf in range(2):
-            gather(v2_s, tab2_s[:].bitcast(U8), idx2, hf)
-        quantize_w1(0, 1, 0, PASS)
-        reorder_w2(w2_w[:].bitcast(U16), w2_w_raw[:].bitcast(U16))
-        reorder_w2(w2_s[:], w2_s_raw[:].bitcast(U8))
+        halves = [slice(0, HALF), slice(HALF, S)]
         prepare_gain()
+        reorder_w2(w2_w[:].bitcast(U16), w2_w_raw[:].bitcast(U16))
         for hf in range(2):
-            gather(v2_w, tab2_w[:].bitcast(U32), idx2, hf)
+            gather(v_w[0, hf][:], tab_w[0][:].bitcast(U32), idx, hf)
+        for hf in range(2):
+            gather(v_s[:, halves[hf]], tab_s[:].bitcast(U8), idx, hf)
+        reorder_w2(w2_s[:], w2_s_raw[:].bitcast(U8))
+        v_w[1, 0] = placed([P, HALF], U32, "v_w10", 512)
+        gather(v_w[1, 0][:], tab_w[1][:].bitcast(U32), idx, 0)
+        w1_s[0, 0] = placed([P, PASS], U8, "w1_s00", 0)
+        quantize_w1(0, 0, 0, PASS)
+        v2_s = held([P, S], U8, "v2_s", tag="w2_s_raw")
+        for hf in range(2):
+            gather(v2_s[:, halves[hf]], tab2_s[:].bitcast(U8), idx2, hf)
+        w1_w[0, 1] = held([P, PASS], U32, "w1_w01", tag="tab2_s")
+        quantize_w1(0, 1, 0, PASS)
+        v2_w = held([P, S], U32, "v2_w", tag="w1_bf")
+        for hf in range(2):
+            gather(v2_w[:, halves[hf]], tab2_w[:].bitcast(U32), idx2, hf)
 
-        w1_bf.append(held([P, 2, PASS * PACK], BF16, "w1_bf1", tag="tab2_w"))
-        whole = [(0, HALF)]
-        split = [(0, HALF // 2), (HALF // 2, HALF)]
-
-        unit(0, 0, whole)
-        for a in range(2):
-            cast_w1(1, a, 0, PASS, False)
-        for a in range(2):
-            quantize_w1(1, a, 0, PASS)
-        unit(0, 1, whole)
-        values00 = similarity(0, 0, 0, HALF)
+        w1_bf.append(placed([P, 2, PASS * PACK], BF16, "w1_bf1", 6144))
+        unit(0, 0)
+        cast_w1(1, 0, 0, PASS, False)
+        cast_w1(1, 1, 0, PASS // 2, False)
+        quantize_w1(1, 0, 0, PASS)
+        cast_w1(1, 1, PASS // 2, PASS, False)
+        quantize_w1(1, 1, 0, P)
+        quantize_w1(1, 1, P, 2 * P)
+        quantize_w1(1, 1, 2 * P, PASS)
+        v_w[1, 1] = placed([P, HALF], U32, "v_w11", 6144)
+        gather(v_w[1, 1][:], tab_w[1][:].bitcast(U32), idx, 1)
+        unit(1, 0)
+        values00 = similarity(0, 0, 0, HALF, False)
         cast_w3(0)
         quantize_h(0, 0, 0, HALF, values00)
-        unit(1, 0, whole)
-        values01 = similarity(0, 1, 0, HALF)
         quantize(w3_w[0][:], w3_s[0][:], w3_bf[0][:])
+        unit(0, 1)
+        values10 = similarity(1, 0, 0, HALF, False)
         cast_w3(1)
-        quantize_h(0, 1, 0, HALF, values01)
-        unit(1, 1, split)
-        values10 = similarity(1, 0, 0, HALF)
-        quantize(w3_w[1][:], w3_s[1][:], w3_bf[1][:])
         quantize_h(1, 0, 0, HALF, values10)
-        score(0, 0, HALF, "ssss")
-        for (lo, hi), engines in zip(split, ("ssss", "vsvs")):
-            values11 = similarity(1, 1, lo, hi)
-            quantize_h(1, 1, lo, hi, values11)
-            score(1, lo, hi, engines)
+        quantize(w3_w[1][:], w3_s[1][:], w3_bf[1][:])
+        unit(1, 1, ((0, HALF),))
+        accs0 = score(0, 0, HALF)
+        values01 = similarity(0, 1, 0, HALF, False)
+        quantize_h(0, 1, 0, HALF, values01)
+        values0 = similarity(1, 1, 0, 256, True)
+        values1 = similarity(1, 1, 256, 512, True)
+        emit(0, 0, HALF, accs0, "ssvv", 1)
+        quantize_h(1, 1, 0, 256, values0)
+        accs_0 = score(1, 0, 256)
+        quantize_h(1, 1, 256, 512, values1)
+        accs_1 = score(1, 256, 512)
+        emit(1, 0, 256, accs_0, "svsv", 2)
+        emit(1, 256, 512, accs_1, "svsv", 2)

@@ -20,8 +20,11 @@ P = 128
 PACK = 4
 PASS = P * PACK
 HALF = 512
-TAB_ROW = (4, 8)
-TINY = 1e-37
+QUARTER = HALF // 2
+QUAD = 32
+TAB_FIRST = (4, 8)
+RUN = 4
+FLOOR_LOG2 = 48
 
 
 def tile_list_visual_rerank_pairs_kernel(
@@ -30,53 +33,54 @@ def tile_list_visual_rerank_pairs_kernel(
     nc = tc.nc
     with ExitStack() as ctx:
         keep = ctx.enter_context(tc.tile_pool(name="keep", bufs=1))
-        shared = ctx.enter_context(tc.tile_pool(name="shared", bufs=1))
-        sq_pool = ctx.enter_context(tc.tile_pool(name="sq", bufs=4))
-        ring = ctx.enter_context(tc.tile_pool(name="ring", bufs=4))
-        psum = ctx.enter_context(tc.psum_pool(name="psum", bufs=8))
+        overlay = ctx.enter_context(tc.tile_pool(name="overlay", bufs=1))
+        psum = ctx.enter_context(tc.psum_pool(name="psum", bufs=1))
 
         def held(shape, dtype, name, tag=None):
             return keep.tile(shape, dtype, name=name, tag=tag or name, align_bytes=64)
 
         def placed(shape, dtype, name, offset):
-            return shared.tile(shape, dtype, name=name, align_bytes=64, offset=offset)
+            return overlay.tile(shape, dtype, name=name, align_bytes=64, offset=offset)
+
+        bf_bytes = PASS * PACK * 2
 
         idx = held([P, S // 16], U16, "idx")
         idx2 = held([P, S // 16], U16, "idx2")
         tab_w = [held([P, T], I32, "tab_w%d" % a) for a in range(2)]
-        tab_s = placed([P, T // 4], I32, "tab_s", 0)
-        tab2_w = placed([P, T2], I32, "tab2_w", 4096)
+        tab_s = held([P, T // 4], I32, "tab_s")
+        tab2_w = held([P, T2], I32, "tab2_w")
         tab2_s = held([P, T2 // 4], I32, "tab2_s")
         w2_w_raw = held([P, H // 2], I32, "w2_w_raw")
         w2_s_raw = held([P, H // 4], I32, "w2_s_raw")
         w2_w = held([P, 2 * H], U8, "w2_w")
         w2_s = held([P, H], U8, "w2_s")
-        v_w = {(0, hf): held([P, HALF], U32, "v_w0%d" % hf) for hf in range(2)}
+        v_w = [held([P, S], U32, "v_w%d" % a) for a in range(2)]
         v_s = held([P, S], U8, "v_s")
+        v2_w = [held([P, HALF], U32, "v2_w0")]
+        v2_s = held([P, S], U8, "v2_s")
         w1_raw = {}
+        w1_bf = [placed([P, 2, PASS * PACK], BF16, "w1_bf0", 0)]
+        w1_w = {(g, a): held([P, PASS], U32, "w1_w%d%d" % (g, a)) for g in range(2) for a in range(2)}
+        w1_s = {(g, a): held([P, PASS], U8, "w1_s%d%d" % (g, a)) for g in range(2) for a in range(2)}
         w3_raw = [held([P, PACK, N], F32, "w3_raw%d" % g) for g in range(2)]
-        w1_bf = [held([P, 2, PASS * PACK], BF16, "w1_bf0", tag="w1_bf")]
-        w1_w = {(g, a): held([P, PASS], U32, "w1_w%d%d" % (g, a)) for g, a in ((0, 0), (1, 0), (1, 1))}
-        w1_s = {(g, a): held([P, PASS], U8, "w1_s%d%d" % (g, a)) for g, a in ((0, 1), (1, 0), (1, 1))}
-        w3_bf = []
         w3_w = [held([P, N], U32, "w3_w%d" % g) for g in range(2)]
         w3_s = [held([P, N], U8, "w3_s%d" % g) for g in range(2)]
         h_w = [held([P, S], U32, "h_w%d" % g) for g in range(2)]
         h_s = [held([P, S], U8, "h_s%d" % g) for g in range(2)]
+        roots = {}
         gain_sb = held([P, 2, PACK], F32, "gain_sb")
         gain_abs = held([P, 2 * PACK], F32, "gain_abs")
         gain_inv = held([P, 2 * PACK], F32, "gain_inv")
-        gain_pos = held([P, 2 * PACK], F32, "gain_pos")
+        gain_twice_pos = held([P, 2 * PACK], F32, "gain_twice_pos")
         gain_sign = held([P, 2 * PACK], F32, "gain_sign")
         bias_sb = held([P, N // P], F32, "bias_sb")
-        warm_in = held([P, 1], F32, "warm_in")
-        warm_out = held([P, 1], F32, "warm_out")
+        floor_arg = held([P, 1], F32, "floor_arg")
+        floor = held([P, 1], F32, "floor")
 
-        nc.vector.memset(warm_in[:], 1.0)
-        nc.scalar.activation(warm_out[:], warm_in[:], ACT.Abs_reciprocal_sqrt)
-        nc.vector.memset(tab_s[:], 0)
-        nc.vector.memset(w2_s_raw[:], 0)
-        nc.vector.memset(tab2_s[:], 0)
+        nc.vector.memset(floor_arg[:], 2.0 ** (2 * FLOOR_LOG2))
+        nc.scalar.activation(floor[:], floor_arg[:], ACT.Abs_reciprocal_sqrt)
+        for plane in (tab_s, w2_s_raw, tab2_s):
+            nc.vector.memset(plane[:], 0)
 
         def load_w1(g, a, lo, hi):
             rows = w1[PASS * a : PASS * (a + 1), PASS * g + lo : PASS * g + hi]
@@ -86,36 +90,55 @@ def tile_list_visual_rerank_pairs_kernel(
         def load_words(tile, words):
             nc.sync.dma_start(tile[:], words.rearrange("p t i -> p (t i)").bitcast(I32))
 
-        for q in range(4):
-            row = 32 * q + TAB_ROW[0]
-            nc.gpsimd.dma_start(tab_s[row : row + 8, :], tab_scales[:, 4 * q : 4 * q + 4, :].bitcast(I32))
-        for r in range(4):
-            nc.gpsimd.dma_start(w2_s_raw[r:P:32, :], w2_scales[0, r:16:4, :].bitcast(I32))
-        for r in range(4):
-            nc.gpsimd.dma_start(tab2_s[r:P:32, :], tab2_scales[0, r:16:4, :].bitcast(I32))
-        with nc.allow_non_contiguous_dma(reason="four gains a partition"):
-            nc.sync.dma_start(gain_sb[:], gain.rearrange("(g p t) -> p g t", g=2, t=PACK))
-        nc.sync.dma_start(w2_w_raw[:], w2_words[0].bitcast(I32))
+        def load_plane(plane, scales):
+            for r in range(PACK):
+                nc.sync.dma_start(plane[r:P:QUAD, :], scales[r : PASS // QUAD : PACK, :].bitcast(I32))
+
         nc.sync.dma_start(idx[:], offs)
+        nc.sync.dma_start(w2_w_raw[:], w2_words[0].bitcast(I32))
+        for q in range(P // QUAD):
+            row = QUAD * q + TAB_FIRST[0]
+            both_passes = tab_scales[:, PACK * q : PACK * (q + 1), :]
+            nc.sync.dma_start(tab_s[row : row + 2 * PACK, :], both_passes.bitcast(I32))
+        with nc.allow_non_contiguous_dma(reason="four gains a partition and group"):
+            nc.sync.dma_start(gain_sb[:], gain.rearrange("(g p t) -> p g t", g=2, t=PACK))
         load_words(tab_w[0], tab_words[0])
         nc.sync.dma_start(idx2[:], offs2)
+        load_plane(w2_s_raw, w2_scales[0])
         load_w1(0, 0, 0, PASS)
+        load_plane(tab2_s, tab2_scales[0])
         load_words(tab_w[1], tab_words[1])
-        load_w1(0, 1, 0, PASS)
         load_words(tab2_w, tab2_words[0])
+        load_w1(0, 1, 0, PASS // 2)
+        load_w1(0, 1, PASS // 2, PASS)
         load_w1(1, 0, 0, PASS)
-        load_w1(1, 1, 0, PASS // 2)
-        load_w1(1, 1, PASS // 2, PASS)
+        load_w1(1, 1, 0, PASS)
         for g in range(2):
             rows = w3[PASS * g : PASS * (g + 1), :]
             nc.sync.dma_start(w3_raw[g][:], rows.rearrange("(p j) n -> p j n", j=PACK))
-        with nc.allow_non_contiguous_dma(reason="one bias a partition"):
+        with nc.allow_non_contiguous_dma(reason="one bias a partition and block of scores"):
             nc.sync.dma_start(bias_sb[:], bias.rearrange("(b p) -> p b", p=P))
 
         def quantize(words, scales, values):
             nc.vector.quantize_mx(out=words.bitcast(FP8X4), scales=scales, in_=values)
 
-        def cast_w1(g, a, lo, hi, on_scalar):
+        def gather(dst, window, offsets):
+            nc.vector.tensor_copy(dst, window.indirect(offsets))
+
+        def prepare_gain():
+            flat = gain_sb[:].rearrange("p g t -> p (g t)")
+            nc.vector.scalar_tensor_tensor(gain_abs[:], flat, -1.0, flat, ALU.mult, ALU.max)
+            nc.vector.tensor_scalar(gain_twice_pos[:], flat, 0.0, 2.0, ALU.is_ge, ALU.mult)
+            nc.vector.tensor_scalar(gain_abs[:], gain_abs[:], floor[:], None, ALU.max)
+            nc.vector.tensor_scalar(gain_sign[:], gain_twice_pos[:], -1.0, None, ALU.add)
+            nc.vector.reciprocal(gain_inv[:], gain_abs[:])
+
+        def reorder_w2(dst, src):
+            nc.vector.tensor_copy(
+                dst.rearrange("p (g t m) -> p g t m", g=2, t=PACK), src.rearrange("p (g m t) -> p g t m", g=2, t=PACK)
+            )
+
+        def round_w1(g, a, lo, hi, on_scalar):
             dst = w1_bf[g][:, a].rearrange("p (t m j) -> p m j t", t=PACK, j=PACK)[:, lo // PACK : hi // PACK]
             src = w1_raw[g, a, lo][:].rearrange("p j (m t) -> p m j t", t=PACK)
             if on_scalar:
@@ -126,54 +149,62 @@ def tile_list_visual_rerank_pairs_kernel(
         def quantize_w1(g, a, lo, hi):
             quantize(w1_w[g, a][:, lo:hi], w1_s[g, a][:, lo:hi], w1_bf[g][:, a, PACK * lo : PACK * hi])
 
-        def cast_w3(g):
-            w3_bf.append(held([P, N * PACK], BF16, "w3_bf%d" % g, tag="root%d0" % g))
-            dst = w3_bf[g][:].rearrange("p (c i j) -> p c j i", i=4, j=PACK)
-            src = w3_raw[g][:].rearrange("p j (c i) -> p c j i", i=4)
-            sign = gain_sign[:, PACK * g : PACK * (g + 1)].unsqueeze(1).unsqueeze(3).broadcast_to([P, N // 4, PACK, 4])
-            nc.vector.tensor_tensor(dst, src, sign, ALU.mult)
+        def round_w3(g, w3_bf):
+            dst = w3_bf[:].rearrange("p (c i j) -> p c j i", i=RUN, j=PACK)
+            src = w3_raw[g][:].rearrange("p j (c i) -> p c j i", i=RUN)
+            sign = gain_sign[:, PACK * g : PACK * (g + 1)].unsqueeze(1).unsqueeze(3)
+            nc.vector.tensor_tensor(dst, src, sign.broadcast_to([P, N // RUN, PACK, RUN]), ALU.mult)
 
-        def gather(dst, window, offsets, hf):
-            nc.vector.tensor_copy(dst, window.indirect(offsets[:, HALF // 16 * hf : HALF // 16 * (hf + 1)]))
-
-        roots = {}
-
-        def difference(g, hf, t):
+        def squared_difference(g, hf, t):
             cols = slice(HALF * hf, HALF * (hf + 1))
             chan = slice(P * t, P * (t + 1))
-            bank = psum.tile([P, HALF], F32, name="bank")
-            for a in range(2):
+            c0 = PASS * g + P * t
+            diff = psum.tile([P, HALF], F32, name="diff", tag="bank%d" % (PACK * hf + t))
+
+            def probe_pass(a):
                 nc.tensor.matmul_mx(
-                    out=bank[:],
+                    out=diff[:],
                     lhsT=w1_w[g, a][:, chan].bitcast(FP8X4),
                     lhsT_scale=w1_s[g, a][:, chan],
-                    rhs=v_w[a, hf][:].bitcast(FP8X4),
-                    rhs_scale=v_s[TAB_ROW[a] : P, cols],
+                    rhs=v_w[a][:, cols].bitcast(FP8X4),
+                    rhs_scale=v_s[TAB_FIRST[a] : P, cols],
                     start=(a == 0),
-                    stop=False,
+                    stop=(a == 1),
                 )
-            c0 = PASS * g + P * t
+
+            probe_pass(0)
             nc.tensor.matmul_mx(
-                out=bank[:],
+                out=diff[:],
                 lhsT=w2_w[:, 2 * c0 : 2 * (c0 + P)].bitcast(FP4X4),
                 lhsT_scale=w2_s[:, c0 : c0 + P],
-                rhs=v2_w[:, cols].bitcast(FP8X4),
+                rhs=v2_w[hf][:].bitcast(FP8X4),
                 rhs_scale=v2_s[:, cols],
                 start=False,
-                stop=True,
+                stop=False,
             )
-            square = sq_pool.tile([P, HALF], F32, name="square")
-            nc.scalar.activation(square[:], bank[:], ACT.Square)
+            probe_pass(1)
+            square = held([P, HALF], F32, "square", tag="square%d" % t)
+            nc.scalar.activation(square[:], diff[:], ACT.Square)
             return square
 
-        def root(g, hf, t, square, lo, hi):
-            col = gain_inv[:, PACK * g + t : PACK * g + t + 1]
-            nc.scalar.activation(roots[g, hf][:, t, lo:hi], square[:, lo:hi], ACT.Abs_reciprocal_sqrt, bias=col, scale=col)
+        def make_roots(g, hf):
+            roots[g, hf] = held([P, PACK, HALF], F32, "root%d%d" % (g, hf))
+            squares = []
 
-        def similarity(g, hf, lo, hi, on_scalar):
-            values = ring.tile([P, (hi - lo) * PACK], BF16, name="values", align_bytes=64)
-            src = roots[g, hf][:, :, lo:hi].rearrange("p t (c i) -> p c t i", i=4)
-            dst = values[:].rearrange("p (c i t) -> p c t i", i=4, t=PACK)
+            def root(t):
+                inv = gain_inv[:, PACK * g + t : PACK * g + t + 1]
+                nc.scalar.activation(roots[g, hf][:, t], squares[t][:], ACT.Abs_reciprocal_sqrt, bias=inv, scale=inv)
+
+            for t in range(PACK):
+                squares.append(squared_difference(g, hf, t))
+                if t > 0:
+                    root(t - 1)
+            root(PACK - 1)
+
+        def similarity(g, hf, lo, hi, on_scalar=False, tag=None):
+            values = held([P, (hi - lo) * PACK], BF16, "values%d%d_%d" % (g, hf, lo), tag=tag)
+            src = roots[g, hf][:, :, lo:hi].rearrange("p t (c i) -> p c t i", i=RUN)
+            dst = values[:].rearrange("p (c i t) -> p c t i", i=RUN, t=PACK)
             if on_scalar:
                 nc.scalar.activation(dst, src, ACT.Square)
             else:
@@ -184,9 +215,9 @@ def tile_list_visual_rerank_pairs_kernel(
             cols = slice(HALF * hf + lo, HALF * hf + hi)
             quantize(h_w[g][:, cols], h_s[g][:, cols], values[:])
 
-        def score(hf, lo, hi):
-            cols = slice(HALF * hf + lo, HALF * hf + hi)
-            accs = [psum.tile([P, hi - lo], F32, name="bank") for b in range(N // P)]
+        def score(cols, first_bank):
+            width = cols.stop - cols.start
+            accs = [psum.tile([P, width], F32, name="acc", tag="bank%d" % (first_bank + b)) for b in range(N // P)]
             for b in range(N // P):
                 for g in range(2):
                     nc.tensor.matmul_mx(
@@ -200,97 +231,69 @@ def tile_list_visual_rerank_pairs_kernel(
                     )
             return accs
 
-        def emit(hf, lo, hi, accs, engines, group):
-            cols = slice(HALF * hf + lo, HALF * hf + hi)
-            staged = held([P, N // P, hi - lo], F32, "scores%d_%d" % (hf, lo))
+        def emit(cols, accs, vector_blocks, blocks_per_store):
+            staged = held([P, N // P, cols.stop - cols.start], F32, "staged%d" % cols.start)
             for b in range(N // P):
-                if engines[b] == "s":
-                    nc.scalar.activation(staged[:, b], accs[b][:], ACT.Identity, bias=bias_sb[:, b : b + 1])
-                else:
+                if b in vector_blocks:
                     nc.vector.tensor_scalar(staged[:, b], accs[b][:], bias_sb[:, b : b + 1], None, ALU.add)
-                if (b + 1) % group == 0:
-                    rows = slice(b + 1 - group, b + 1)
-                    nc.sync.dma_start(out.rearrange("(b p) s -> p b s", p=P)[:, rows, cols], staged[:, rows])
+                else:
+                    nc.scalar.activation(staged[:, b], accs[b][:], ACT.Identity, bias=bias_sb[:, b : b + 1])
+                if (b + 1) % blocks_per_store == 0:
+                    blocks = slice(b + 1 - blocks_per_store, b + 1)
+                    nc.sync.dma_start(out.rearrange("(b p) s -> p b s", p=P)[:, blocks, cols], staged[:, blocks])
 
-        def unit(g, hf, pieces=((0, HALF),)):
-            roots[g, hf] = held([P, PACK, HALF], F32, "root%d%d" % (g, hf))
-            squares = []
-            for t in range(PACK):
-                squares.append(difference(g, hf, t))
-                if t > 0:
-                    root(g, hf, t - 1, squares[t - 1], *pieces[0])
-            root(g, hf, PACK - 1, squares[PACK - 1], *pieces[0])
-            for lo, hi in pieces[1:]:
-                for t in range(PACK):
-                    root(g, hf, t, squares[t], lo, hi)
-
-        def prepare_gain():
-            gain_flat = gain_sb[:].rearrange("p g t -> p (g t)")
-            nc.vector.scalar_tensor_tensor(gain_abs[:], gain_flat, -1.0, gain_flat, ALU.mult, ALU.max)
-            nc.vector.tensor_scalar(gain_pos[:], gain_flat, 0.0, 2.0, ALU.is_ge, ALU.mult)
-            nc.vector.tensor_scalar(gain_abs[:], gain_abs[:], TINY, None, ALU.max)
-            nc.vector.tensor_scalar(gain_sign[:], gain_pos[:], -1.0, None, ALU.add)
-            nc.vector.reciprocal(gain_inv[:], gain_abs[:])
-
-        def reorder_w2(dst, src):
-            nc.vector.tensor_copy(
-                dst.rearrange("p (g t m) -> p g t m", g=2, t=PACK), src.rearrange("p (g m t) -> p g t m", g=2, t=PACK)
-            )
-
-        for a in range(2):
-            cast_w1(0, a, 0, PASS, True)
-        halves = [slice(0, HALF), slice(HALF, S)]
-        prepare_gain()
+        round_w1(0, 0, 0, PASS, on_scalar=True)
+        round_w1(0, 1, 0, PASS // 2, on_scalar=True)
         reorder_w2(w2_w[:].bitcast(U16), w2_w_raw[:].bitcast(U16))
-        for hf in range(2):
-            gather(v_w[0, hf][:], tab_w[0][:].bitcast(U32), idx, hf)
-        for hf in range(2):
-            gather(v_s[:, halves[hf]], tab_s[:].bitcast(U8), idx, hf)
+        prepare_gain()
+        gather(v_s[:], tab_s[:].bitcast(U8), idx[:])
+        gather(v_w[0][:], tab_w[0][:].bitcast(U32), idx[:])
         reorder_w2(w2_s[:], w2_s_raw[:].bitcast(U8))
-        v_w[1, 0] = placed([P, HALF], U32, "v_w10", 512)
-        gather(v_w[1, 0][:], tab_w[1][:].bitcast(U32), idx, 0)
-        w1_s[0, 0] = placed([P, PASS], U8, "w1_s00", 0)
+        gather(v2_s[:], tab2_s[:].bitcast(U8), idx2[:])
+        gather(v_w[1][:], tab_w[1][:].bitcast(U32), idx[:])
         quantize_w1(0, 0, 0, PASS)
-        v2_s = held([P, S], U8, "v2_s", tag="w2_s_raw")
-        for hf in range(2):
-            gather(v2_s[:, halves[hf]], tab2_s[:].bitcast(U8), idx2, hf)
-        w1_w[0, 1] = held([P, PASS], U32, "w1_w01", tag="tab2_s")
-        quantize_w1(0, 1, 0, PASS)
-        v2_w = held([P, S], U32, "v2_w", tag="w1_bf")
-        for hf in range(2):
-            gather(v2_w[:, halves[hf]], tab2_w[:].bitcast(U32), idx2, hf)
+        gather(v2_w[0][:], tab2_w[:].bitcast(U32), idx2[:, : HALF // 16])
+        round_w1(0, 1, PASS // 2, PASS, on_scalar=False)
+        for lo, hi in ((0, P), (P, 2 * P), (2 * P, PASS)):
+            quantize_w1(0, 1, lo, hi)
 
-        w1_bf.append(placed([P, 2, PASS * PACK], BF16, "w1_bf1", 6144))
-        unit(0, 0)
-        cast_w1(1, 0, 0, PASS, False)
-        cast_w1(1, 1, 0, PASS // 2, False)
-        quantize_w1(1, 0, 0, PASS)
-        cast_w1(1, 1, PASS // 2, PASS, False)
-        quantize_w1(1, 1, 0, P)
-        quantize_w1(1, 1, P, 2 * P)
-        quantize_w1(1, 1, 2 * P, PASS)
-        v_w[1, 1] = placed([P, HALF], U32, "v_w11", 6144)
-        gather(v_w[1, 1][:], tab_w[1][:].bitcast(U32), idx, 1)
-        unit(1, 0)
-        values00 = similarity(0, 0, 0, HALF, False)
-        cast_w3(0)
+        w1_bf.append(placed([P, 2, PASS * PACK], BF16, "w1_bf1", bf_bytes))
+        make_roots(0, 0)
+        v2_w.append(placed([P, HALF], U32, "v2_w1", 0))
+        gather(v2_w[1][:], tab2_w[:].bitcast(U32), idx2[:, HALF // 16 :])
+        make_roots(0, 1)
+        for a in range(2):
+            round_w1(1, a, 0, PASS, on_scalar=False)
+        for a in range(2):
+            quantize_w1(1, a, 0, PASS)
+        make_roots(1, 0)
+
+        w3_bf0 = placed([P, N * PACK], BF16, "w3_bf0", bf_bytes)
+        round_w3(0, w3_bf0)
+        values00 = similarity(0, 0, 0, HALF, tag="w3_raw0")
+        quantize(w3_w[0][:], w3_s[0][:], w3_bf0[:])
+        w3_bf1 = held([P, N * PACK], BF16, "w3_bf1", tag="root00")
+        round_w3(1, w3_bf1)
         quantize_h(0, 0, 0, HALF, values00)
-        quantize(w3_w[0][:], w3_s[0][:], w3_bf[0][:])
-        unit(0, 1)
-        values10 = similarity(1, 0, 0, HALF, False)
-        cast_w3(1)
+        quantize(w3_w[1][:], w3_s[1][:], w3_bf1[:])
+        values01_front = similarity(0, 1, 0, QUARTER, tag="w3_raw1")
+        quantize_h(0, 1, 0, QUARTER, values01_front)
+        values10 = similarity(1, 0, 0, HALF)
         quantize_h(1, 0, 0, HALF, values10)
-        quantize(w3_w[1][:], w3_s[1][:], w3_bf[1][:])
-        unit(1, 1, ((0, HALF),))
-        accs0 = score(0, 0, HALF)
-        values01 = similarity(0, 1, 0, HALF, False)
-        quantize_h(0, 1, 0, HALF, values01)
-        values0 = similarity(1, 1, 0, 256, True)
-        values1 = similarity(1, 1, 256, 512, True)
-        emit(0, 0, HALF, accs0, "ssvv", 1)
-        quantize_h(1, 1, 0, 256, values0)
-        accs_0 = score(1, 0, 256)
-        quantize_h(1, 1, 256, 512, values1)
-        accs_1 = score(1, 256, 512)
-        emit(1, 0, 256, accs_0, "svsv", 2)
-        emit(1, 256, 512, accs_1, "svsv", 2)
+        make_roots(1, 1)
+        first_half = slice(0, HALF)
+        accs_first = score(first_half, 0)
+        values01_back = similarity(0, 1, QUARTER, HALF, tag="root10")
+        quantize_h(0, 1, QUARTER, HALF, values01_back)
+        emit(first_half, accs_first, vector_blocks=(), blocks_per_store=1)
+
+        third_quarter = slice(HALF, HALF + QUARTER)
+        last_quarter = slice(HALF + QUARTER, S)
+        values11_front = similarity(1, 1, 0, QUARTER)
+        values11_back = similarity(1, 1, QUARTER, HALF, on_scalar=True)
+        quantize_h(1, 1, 0, QUARTER, values11_front)
+        accs_third = score(third_quarter, PACK)
+        quantize_h(1, 1, QUARTER, HALF, values11_back)
+        accs_last = score(last_quarter, 0)
+        emit(third_quarter, accs_third, vector_blocks=(1, 3), blocks_per_store=2)
+        emit(last_quarter, accs_last, vector_blocks=(1, 3), blocks_per_store=2)

from contextlib import ExitStack

import concourse.mybir as mybir

K, K2, H, N, T, T2, S = 1024, 512, 1024, 512, 2048, 4096, 1024
FLOPS = 2 * S * (K * H + K2 * H + H * N)

F32 = mybir.dt.float32
BF16 = mybir.dt.bfloat16
I32 = mybir.dt.int32
U32 = mybir.dt.uint32
U16 = mybir.dt.uint16
U8 = mybir.dt.uint8
FP8X4 = mybir.dt.float8_e4m3fn_x4
FP4X4 = mybir.dt.float4_e2m1fn_x4
ALU = mybir.AluOpType
ACT = mybir.ActivationFunctionType

P = 128
PACK = 4
PASS = P * PACK
HALF = 512
QUARTER = HALF // 2
QUAD = 32
TAB_FIRST = (4, 8)
RUN = 4
FLOOR_LOG2 = 48


def tile_list_visual_rerank_pairs_kernel(
    tc, tab_words, tab_scales, offs, tab2_words, tab2_scales, offs2, w1, w2_words, w2_scales, gain, w3, bias, out
):
    nc = tc.nc
    with ExitStack() as ctx:
        keep = ctx.enter_context(tc.tile_pool(name="keep", bufs=1))
        overlay = ctx.enter_context(tc.tile_pool(name="overlay", bufs=1))
        psum = ctx.enter_context(tc.psum_pool(name="psum", bufs=1))

        def held(shape, dtype, name, tag=None):
            return keep.tile(shape, dtype, name=name, tag=tag or name, align_bytes=64)

        def placed(shape, dtype, name, offset):
            return overlay.tile(shape, dtype, name=name, align_bytes=64, offset=offset)

        bf_bytes = PASS * PACK * 2

        idx = held([P, S // 16], U16, "idx")
        idx2 = held([P, S // 16], U16, "idx2")
        tab_w = [held([P, T], I32, "tab_w%d" % a) for a in range(2)]
        tab_s = held([P, T // 4], I32, "tab_s")
        tab2_w = held([P, T2], I32, "tab2_w")
        tab2_s = held([P, T2 // 4], I32, "tab2_s")
        w2_w_raw = held([P, H // 2], I32, "w2_w_raw")
        w2_s_raw = held([P, H // 4], I32, "w2_s_raw")
        w2_w = held([P, 2 * H], U8, "w2_w")
        w2_s = held([P, H], U8, "w2_s")
        v_w = [held([P, S], U32, "v_w%d" % a) for a in range(2)]
        v_s = held([P, S], U8, "v_s")
        v2_w = [held([P, HALF], U32, "v2_w0")]
        v2_s = held([P, S], U8, "v2_s")
        w1_raw = {}
        w1_bf = [placed([P, 2, PASS * PACK], BF16, "w1_bf0", 0)]
        w1_w = {(g, a): held([P, PASS], U32, "w1_w%d%d" % (g, a)) for g in range(2) for a in range(2)}
        w1_s = {(g, a): held([P, PASS], U8, "w1_s%d%d" % (g, a)) for g in range(2) for a in range(2)}
        w3_raw = [held([P, PACK, N], F32, "w3_raw%d" % g) for g in range(2)]
        w3_w = [held([P, N], U32, "w3_w%d" % g) for g in range(2)]
        w3_s = [held([P, N], U8, "w3_s%d" % g) for g in range(2)]
        h_w = [held([P, S], U32, "h_w%d" % g) for g in range(2)]
        h_s = [held([P, S], U8, "h_s%d" % g) for g in range(2)]
        roots = {}
        gain_sb = held([P, 2, PACK], F32, "gain_sb")
        gain_abs = held([P, 2 * PACK], F32, "gain_abs")
        gain_inv = held([P, 2 * PACK], F32, "gain_inv")
        gain_twice_pos = held([P, 2 * PACK], F32, "gain_twice_pos")
        gain_sign = held([P, 2 * PACK], F32, "gain_sign")
        bias_sb = held([P, N // P], F32, "bias_sb")
        floor_arg = held([P, 1], F32, "floor_arg")
        floor = held([P, 1], F32, "floor")

        nc.vector.memset(floor_arg[:], 2.0 ** (2 * FLOOR_LOG2))
        nc.scalar.activation(floor[:], floor_arg[:], ACT.Abs_reciprocal_sqrt)
        for plane in (tab_s, w2_s_raw, tab2_s):
            nc.vector.memset(plane[:], 0)

        def load_w1(g, a, lo, hi):
            rows = w1[PASS * a : PASS * (a + 1), PASS * g + lo : PASS * g + hi]
            w1_raw[g, a, lo] = held([P, PACK, hi - lo], F32, "w1_raw%d%d_%d" % (g, a, lo))
            nc.sync.dma_start(w1_raw[g, a, lo][:], rows.rearrange("(p j) c -> p j c", j=PACK))

        def load_words(tile, words):
            nc.sync.dma_start(tile[:], words.rearrange("p t i -> p (t i)").bitcast(I32))

        def load_plane(plane, scales):
            for r in range(PACK):
                nc.sync.dma_start(plane[r:P:QUAD, :], scales[r : PASS // QUAD : PACK, :].bitcast(I32))

        nc.sync.dma_start(idx[:], offs)
        nc.sync.dma_start(w2_w_raw[:], w2_words[0].bitcast(I32))
        for q in range(P // QUAD):
            row = QUAD * q + TAB_FIRST[0]
            both_passes = tab_scales[:, PACK * q : PACK * (q + 1), :]
            nc.sync.dma_start(tab_s[row : row + 2 * PACK, :], both_passes.bitcast(I32))
        with nc.allow_non_contiguous_dma(reason="four gains a partition and group"):
            nc.sync.dma_start(gain_sb[:], gain.rearrange("(g p t) -> p g t", g=2, t=PACK))
        load_words(tab_w[0], tab_words[0])
        nc.sync.dma_start(idx2[:], offs2)
        load_plane(w2_s_raw, w2_scales[0])
        load_w1(0, 0, 0, PASS)
        load_plane(tab2_s, tab2_scales[0])
        load_words(tab_w[1], tab_words[1])
        load_words(tab2_w, tab2_words[0])
        load_w1(0, 1, 0, PASS // 2)
        load_w1(0, 1, PASS // 2, PASS)
        load_w1(1, 0, 0, PASS)
        load_w1(1, 1, 0, PASS)
        for g in range(2):
            rows = w3[PASS * g : PASS * (g + 1), :]
            nc.sync.dma_start(w3_raw[g][:], rows.rearrange("(p j) n -> p j n", j=PACK))
        with nc.allow_non_contiguous_dma(reason="one bias a partition and block of scores"):
            nc.sync.dma_start(bias_sb[:], bias.rearrange("(b p) -> p b", p=P))

        def quantize(words, scales, values):
            nc.vector.quantize_mx(out=words.bitcast(FP8X4), scales=scales, in_=values)

        def gather(dst, window, offsets):
            nc.vector.tensor_copy(dst, window.indirect(offsets))

        def prepare_gain():
            flat = gain_sb[:].rearrange("p g t -> p (g t)")
            nc.vector.scalar_tensor_tensor(gain_abs[:], flat, -1.0, flat, ALU.mult, ALU.max)
            nc.vector.tensor_scalar(gain_twice_pos[:], flat, 0.0, 2.0, ALU.is_ge, ALU.mult)
            nc.vector.tensor_scalar(gain_abs[:], gain_abs[:], floor[:], None, ALU.max)
            nc.vector.tensor_scalar(gain_sign[:], gain_twice_pos[:], -1.0, None, ALU.add)
            nc.vector.reciprocal(gain_inv[:], gain_abs[:])

        def reorder_w2(dst, src):
            nc.vector.tensor_copy(
                dst.rearrange("p (g t m) -> p g t m", g=2, t=PACK), src.rearrange("p (g m t) -> p g t m", g=2, t=PACK)
            )

        def round_w1(g, a, lo, hi, on_scalar):
            dst = w1_bf[g][:, a].rearrange("p (t m j) -> p m j t", t=PACK, j=PACK)[:, lo // PACK : hi // PACK]
            src = w1_raw[g, a, lo][:].rearrange("p j (m t) -> p m j t", t=PACK)
            if on_scalar:
                nc.scalar.activation(dst, src, ACT.Copy, scale=-1.0)
            else:
                nc.vector.tensor_scalar(dst, src, -1.0, None, ALU.mult)

        def quantize_w1(g, a, lo, hi):
            quantize(w1_w[g, a][:, lo:hi], w1_s[g, a][:, lo:hi], w1_bf[g][:, a, PACK * lo : PACK * hi])

        def round_w3(g, w3_bf):
            dst = w3_bf[:].rearrange("p (c i j) -> p c j i", i=RUN, j=PACK)
            src = w3_raw[g][:].rearrange("p j (c i) -> p c j i", i=RUN)
            sign = gain_sign[:, PACK * g : PACK * (g + 1)].unsqueeze(1).unsqueeze(3)
            nc.vector.tensor_tensor(dst, src, sign.broadcast_to([P, N // RUN, PACK, RUN]), ALU.mult)

        def squared_difference(g, hf, t):
            cols = slice(HALF * hf, HALF * (hf + 1))
            chan = slice(P * t, P * (t + 1))
            c0 = PASS * g + P * t
            diff = psum.tile([P, HALF], F32, name="diff", tag="bank%d" % (PACK * hf + t))

            def probe_pass(a):
                nc.tensor.matmul_mx(
                    out=diff[:],
                    lhsT=w1_w[g, a][:, chan].bitcast(FP8X4),
                    lhsT_scale=w1_s[g, a][:, chan],
                    rhs=v_w[a][:, cols].bitcast(FP8X4),
                    rhs_scale=v_s[TAB_FIRST[a] : P, cols],
                    start=(a == 0),
                    stop=(a == 1),
                )

            probe_pass(0)
            nc.tensor.matmul_mx(
                out=diff[:],
                lhsT=w2_w[:, 2 * c0 : 2 * (c0 + P)].bitcast(FP4X4),
                lhsT_scale=w2_s[:, c0 : c0 + P],
                rhs=v2_w[hf][:].bitcast(FP8X4),
                rhs_scale=v2_s[:, cols],
                start=False,
                stop=False,
            )
            probe_pass(1)
            square = held([P, HALF], F32, "square", tag="square%d" % t)
            nc.scalar.activation(square[:], diff[:], ACT.Square)
            return square

        def make_roots(g, hf):
            roots[g, hf] = held([P, PACK, HALF], F32, "root%d%d" % (g, hf))
            squares = []

            def root(t):
                inv = gain_inv[:, PACK * g + t : PACK * g + t + 1]
                nc.scalar.activation(roots[g, hf][:, t], squares[t][:], ACT.Abs_reciprocal_sqrt, bias=inv, scale=inv)

            for t in range(PACK):
                squares.append(squared_difference(g, hf, t))
                if t > 0:
                    root(t - 1)
            root(PACK - 1)

        def similarity(g, hf, lo, hi, on_scalar=False, tag=None):
            values = held([P, (hi - lo) * PACK], BF16, "values%d%d_%d" % (g, hf, lo), tag=tag)
            src = roots[g, hf][:, :, lo:hi].rearrange("p t (c i) -> p c t i", i=RUN)
            dst = values[:].rearrange("p (c i t) -> p c t i", i=RUN, t=PACK)
            if on_scalar:
                nc.scalar.activation(dst, src, ACT.Square)
            else:
                nc.vector.tensor_tensor(dst, src, src, ALU.mult)
            return values

        def quantize_h(g, hf, lo, hi, values):
            cols = slice(HALF * hf + lo, HALF * hf + hi)
            quantize(h_w[g][:, cols], h_s[g][:, cols], values[:])

        def score(cols, first_bank):
            width = cols.stop - cols.start
            accs = [psum.tile([P, width], F32, name="acc", tag="bank%d" % (first_bank + b)) for b in range(N // P)]
            for b in range(N // P):
                for g in range(2):
                    nc.tensor.matmul_mx(
                        out=accs[b][:],
                        lhsT=w3_w[g][:, P * b : P * (b + 1)].bitcast(FP8X4),
                        lhsT_scale=w3_s[g][:, P * b : P * (b + 1)],
                        rhs=h_w[g][:, cols].bitcast(FP8X4),
                        rhs_scale=h_s[g][:, cols],
                        start=(g == 0),
                        stop=(g == 1),
                    )
            return accs

        def emit(cols, accs, vector_blocks, blocks_per_store):
            staged = held([P, N // P, cols.stop - cols.start], F32, "staged%d" % cols.start)
            for b in range(N // P):
                if b in vector_blocks:
                    nc.vector.tensor_scalar(staged[:, b], accs[b][:], bias_sb[:, b : b + 1], None, ALU.add)
                else:
                    nc.scalar.activation(staged[:, b], accs[b][:], ACT.Identity, bias=bias_sb[:, b : b + 1])
                if (b + 1) % blocks_per_store == 0:
                    blocks = slice(b + 1 - blocks_per_store, b + 1)
                    nc.sync.dma_start(out.rearrange("(b p) s -> p b s", p=P)[:, blocks, cols], staged[:, blocks])

        round_w1(0, 0, 0, PASS, on_scalar=True)
        round_w1(0, 1, 0, PASS // 2, on_scalar=True)
        reorder_w2(w2_w[:].bitcast(U16), w2_w_raw[:].bitcast(U16))
        prepare_gain()
        gather(v_s[:], tab_s[:].bitcast(U8), idx[:])
        gather(v_w[0][:], tab_w[0][:].bitcast(U32), idx[:])
        reorder_w2(w2_s[:], w2_s_raw[:].bitcast(U8))
        gather(v2_s[:], tab2_s[:].bitcast(U8), idx2[:])
        gather(v_w[1][:], tab_w[1][:].bitcast(U32), idx[:])
        quantize_w1(0, 0, 0, PASS)
        gather(v2_w[0][:], tab2_w[:].bitcast(U32), idx2[:, : HALF // 16])
        round_w1(0, 1, PASS // 2, PASS, on_scalar=False)
        for lo, hi in ((0, P), (P, 2 * P), (2 * P, PASS)):
            quantize_w1(0, 1, lo, hi)

        w1_bf.append(placed([P, 2, PASS * PACK], BF16, "w1_bf1", bf_bytes))
        make_roots(0, 0)
        v2_w.append(placed([P, HALF], U32, "v2_w1", 0))
        gather(v2_w[1][:], tab2_w[:].bitcast(U32), idx2[:, HALF // 16 :])
        make_roots(0, 1)
        for a in range(2):
            round_w1(1, a, 0, PASS, on_scalar=False)
        for a in range(2):
            quantize_w1(1, a, 0, PASS)
        make_roots(1, 0)

        w3_bf0 = placed([P, N * PACK], BF16, "w3_bf0", bf_bytes)
        round_w3(0, w3_bf0)
        values00 = similarity(0, 0, 0, HALF, tag="w3_raw0")
        quantize(w3_w[0][:], w3_s[0][:], w3_bf0[:])
        w3_bf1 = held([P, N * PACK], BF16, "w3_bf1", tag="root00")
        round_w3(1, w3_bf1)
        quantize_h(0, 0, 0, HALF, values00)
        quantize(w3_w[1][:], w3_s[1][:], w3_bf1[:])
        values01_front = similarity(0, 1, 0, QUARTER, tag="w3_raw1")
        quantize_h(0, 1, 0, QUARTER, values01_front)
        values10 = similarity(1, 0, 0, HALF)
        quantize_h(1, 0, 0, HALF, values10)
        make_roots(1, 1)
        first_half = slice(0, HALF)
        accs_first = score(first_half, 0)
        values01_back = similarity(0, 1, QUARTER, HALF, tag="root10")
        quantize_h(0, 1, QUARTER, HALF, values01_back)
        emit(first_half, accs_first, vector_blocks=(), blocks_per_store=1)

        third_quarter = slice(HALF, HALF + QUARTER)
        last_quarter = slice(HALF + QUARTER, S)
        values11_front = similarity(1, 1, 0, QUARTER)
        values11_back = similarity(1, 1, QUARTER, HALF, on_scalar=True)
        quantize_h(1, 1, 0, QUARTER, values11_front)
        accs_third = score(third_quarter, PACK)
        quantize_h(1, 1, QUARTER, HALF, values11_back)
        accs_last = score(last_quarter, 0)
        emit(third_quarter, accs_third, vector_blocks=(1, 3), blocks_per_store=2)
        emit(last_quarter, accs_last, vector_blocks=(1, 3), blocks_per_store=2)
